import numpy as np
import ml_dtypes

BF16 = ml_dtypes.bfloat16


def bf(x):
    return np.asarray(x, np.float32).astype(BF16)


def f32(x):
    return np.asarray(x, np.float32)


def f64(x):
    return np.asarray(x).astype(np.float64)


def striped(idx):
    return np.tile(idx.reshape(-1, 16).T, (8, 1))


S, K, H, M, N, E, Q = 512, 256, 256, 128, 128, 1, 128


def sigmoid(v):
    return 1.0 / (1.0 + np.exp(-v))


def setup_inputs():
    return {"base": bf(np.random.standard_normal((M, S))), "x": bf(np.random.standard_normal((K, N))), "w": bf(np.random.standard_normal((E, K, H)) / np.sqrt(K)), "b": f32(0.5 * np.random.standard_normal((H, E))), "w2": bf(1.5 * np.random.standard_normal((E, H, M)) / np.sqrt(H)), "c": f32(0.2 + 0.8 * np.random.random_sample((1, N))), "offs": striped(np.random.permutation(S)[:N])}


def reference(base, x, w, b, w2, c, offs):
    idx = offs[:16].T.reshape(-1)
    z = f64(base).copy()
    for e in range(E):
        t = f64(w)[e].T @ f64(x)[:, e * Q : (e + 1) * Q] + f64(b)[:, e : e + 1]
        t = t * sigmoid(t) * f64(c)[:, e * Q : (e + 1) * Q]
        z[:, idx[e * Q : (e + 1) * Q]] += f64(w2)[e].T @ t
    return z

@@ -1,0 +1,70 @@
+import concourse.mybir as mybir
+from concourse.masks import make_identity
+
+BF16, F32, U16 = mybir.dt.bfloat16, mybir.dt.float32, mybir.dt.uint16
+SILU = mybir.ActivationFunctionType.Silu
+MULT = mybir.AluOpType.mult
+
+P = 128
+TOKENS = 512
+ENTRIES = 128
+HIDDEN = 256
+BLOCKS = 2
+
+FLOPS = 2 * 256 * HIDDEN * ENTRIES + 2 * HIDDEN * P * ENTRIES
+
+
+def tile_rows_ffnback_silu_kernel(tc, base, x, w, b, w2, c, offs, out):
+    nc = tc.nc
+    with (
+        tc.tile_pool(name="held", bufs=1) as held,
+        tc.psum_pool(name="psum", bufs=1) as psum,
+    ):
+        w_tile = held.tile([P, BLOCKS, HIDDEN], BF16, name="w_tile")
+        nc.sync.dma_start(w_tile[:], w.rearrange("e (p a) h -> p (e a) h", a=BLOCKS))
+        x_tile = held.tile([P, BLOCKS, ENTRIES], BF16, name="x_tile")
+        nc.sync.dma_start(x_tile[:], x.rearrange("(p a) n -> p a n", a=BLOCKS))
+        b_tile = held.tile([P, BLOCKS], F32, name="b_tile")
+        nc.scalar.dma_start(b_tile[:], b.rearrange("(a p) o -> p (a o)", p=P))
+        c_tile = held.tile([P, ENTRIES], F32, name="c_tile")
+        nc.scalar.dma_start(c_tile[:], c.rearrange("o n -> (o n)").partition_broadcast(P))
+        base_tile = held.tile([P, TOKENS], BF16, name="base_tile")
+        nc.sync.dma_start(base_tile[:], base)
+        w2_tile = held.tile([P, BLOCKS, P], BF16, name="w2_tile")
+        nc.sync.dma_start(w2_tile[:], w2.rearrange("e (a p) m -> p (e a) m", p=P))
+        offsets = held.tile([P, ENTRIES // 16], U16, name="offsets")
+        nc.sync.dma_start(offsets[:], offs)
+
+        identity = held.tile([P, P], BF16, name="identity")
+        make_identity(nc, identity[:])
+
+        hidden = held.tile([P, BLOCKS, ENTRIES], BF16, name="hidden")
+        for i in range(BLOCKS):
+            pre = psum.tile([P, ENTRIES], F32, name=f"pre{i}")
+            for k in range(BLOCKS):
+                nc.tensor.matmul(
+                    pre[:],
+                    w_tile[:, k, i * P : (i + 1) * P],
+                    x_tile[:, k, :],
+                    start=(k == 0),
+                    stop=(k == BLOCKS - 1),
+                )
+            act = held.tile([P, ENTRIES], F32, name=f"act{i}")
+            nc.scalar.activation(act[:], pre[:], SILU, bias=b_tile[:, i : i + 1])
+            nc.vector.tensor_tensor(hidden[:, i, :], act[:], c_tile[:], MULT)
+
+        window = psum.tile([P, TOKENS], F32, name="window")
+        nc.tensor.matmul(window[:], identity[:], base_tile[:], start=True, stop=False)
+
+        for i in range(BLOCKS):
+            nc.tensor.matmul(
+                window[:].indirect(offsets[:]),
+                w2_tile[:, i, :],
+                hidden[:, i, :],
+                start=False,
+                stop=(i == BLOCKS - 1),
+            )
+
+        z_tile = held.tile([P, TOKENS], F32, name="z_tile")
+        nc.vector.tensor_copy(z_tile[:], window[:])
+        nc.sync.dma_start(out, z_tile[:])

@@ -24,10 +24,10 @@ def tile_rows_ffnback_silu_kernel(tc, base, x, w, b, w2, c, offs, out):
         nc.sync.dma_start(w_tile[:], w.rearrange("e (p a) h -> p (e a) h", a=BLOCKS))
         x_tile = held.tile([P, BLOCKS, ENTRIES], BF16, name="x_tile")
         nc.sync.dma_start(x_tile[:], x.rearrange("(p a) n -> p a n", a=BLOCKS))
-        b_tile = held.tile([P, BLOCKS], F32, name="b_tile")
-        nc.scalar.dma_start(b_tile[:], b.rearrange("(a p) o -> p (a o)", p=P))
-        c_tile = held.tile([P, ENTRIES], F32, name="c_tile")
-        nc.scalar.dma_start(c_tile[:], c.rearrange("o n -> (o n)").partition_broadcast(P))
+        b_row = held.tile([1, HIDDEN], F32, name="b_row")
+        nc.scalar.dma_start(b_row[:], b.rearrange("h o -> o h"))
+        c_row = held.tile([1, ENTRIES], F32, name="c_row")
+        nc.scalar.dma_start(c_row[:], c)
         base_tile = held.tile([P, TOKENS], BF16, name="base_tile")
         nc.sync.dma_start(base_tile[:], base)
         w2_tile = held.tile([P, BLOCKS, P], BF16, name="w2_tile")
@@ -38,20 +38,27 @@ def tile_rows_ffnback_silu_kernel(tc, base, x, w, b, w2, c, offs, out):
         identity = held.tile([P, P], BF16, name="identity")
         make_identity(nc, identity[:])
 
+        ones = held.tile([1, P], F32, name="ones")
+        nc.vector.memset(ones[:], 1.0)
+
+        c_all = psum.tile([P, ENTRIES], F32, name="c_all")
+        nc.tensor.matmul(c_all[:], ones[:], c_row[:], start=True, stop=True)
+
         hidden = held.tile([P, BLOCKS, ENTRIES], BF16, name="hidden")
         for i in range(BLOCKS):
             pre = psum.tile([P, ENTRIES], F32, name=f"pre{i}")
+            nc.tensor.matmul(pre[:], b_row[:, i * P : (i + 1) * P], ones[:], start=True, stop=False)
             for k in range(BLOCKS):
                 nc.tensor.matmul(
                     pre[:],
                     w_tile[:, k, i * P : (i + 1) * P],
                     x_tile[:, k, :],
-                    start=(k == 0),
+                    start=False,
                     stop=(k == BLOCKS - 1),
                 )
             act = held.tile([P, ENTRIES], F32, name=f"act{i}")
-            nc.scalar.activation(act[:], pre[:], SILU, bias=b_tile[:, i : i + 1])
-            nc.vector.tensor_tensor(hidden[:, i, :], act[:], c_tile[:], MULT)
+            nc.scalar.activation(act[:], pre[:], SILU)
+            nc.vector.tensor_tensor(hidden[:, i, :], act[:], c_all[:], MULT)
 
         window = psum.tile([P, TOKENS], F32, name="window")
         nc.tensor.matmul(window[:], identity[:], base_tile[:], start=True, stop=False)

@@ -9,6 +9,7 @@ P = 128
 TOKENS = 512
 ENTRIES = 128
 HIDDEN = 256
+WARM_UPS = 3
 BLOCKS = 2
 
 FLOPS = 2 * 256 * HIDDEN * ENTRIES + 2 * HIDDEN * P * ENTRIES
@@ -41,23 +42,39 @@ def tile_rows_ffnback_silu_kernel(tc, base, x, w, b, w2, c, offs, out):
         ones = held.tile([1, P], F32, name="ones")
         nc.vector.memset(ones[:], 1.0)
 
+        early = held.tile([1, P], F32, name="early")
+        nc.scalar.activation(early[:], ones[:], SILU)
+
+        b_columns = psum.tile([P, BLOCKS], F32, name="b_columns")
+        for i in range(BLOCKS):
+            nc.tensor.matmul(
+                b_columns[:, i : i + 1], b_row[:, i * P : (i + 1) * P], ones[:, 0:1], start=True, stop=True
+            )
+        b_tile = held.tile([P, BLOCKS], F32, name="b_tile")
+        nc.vector.tensor_copy(b_tile[:], b_columns[:])
+
+        zeros = held.tile([P, TOKENS], BF16, name="zeros")
+        nc.vector.memset(zeros[:], 0.0)
+        warm = psum.tile([P, TOKENS], F32, name="warm")
+        for step in range(WARM_UPS):
+            nc.tensor.matmul(warm[:], zeros[:, 0:P], zeros[:], start=True, stop=True)
+
         c_all = psum.tile([P, ENTRIES], F32, name="c_all")
         nc.tensor.matmul(c_all[:], ones[:], c_row[:], start=True, stop=True)
 
         hidden = held.tile([P, BLOCKS, ENTRIES], BF16, name="hidden")
         for i in range(BLOCKS):
             pre = psum.tile([P, ENTRIES], F32, name=f"pre{i}")
-            nc.tensor.matmul(pre[:], b_row[:, i * P : (i + 1) * P], ones[:], start=True, stop=False)
             for k in range(BLOCKS):
                 nc.tensor.matmul(
                     pre[:],
                     w_tile[:, k, i * P : (i + 1) * P],
                     x_tile[:, k, :],
-                    start=False,
+                    start=(k == 0),
                     stop=(k == BLOCKS - 1),
                 )
             act = held.tile([P, ENTRIES], F32, name=f"act{i}")
-            nc.scalar.activation(act[:], pre[:], SILU)
+            nc.scalar.activation(act[:], pre[:], SILU, bias=b_tile[:, i : i + 1])
             nc.vector.tensor_tensor(hidden[:, i, :], act[:], c_all[:], MULT)
 
         window = psum.tile([P, TOKENS], F32, name="window")

import concourse.mybir as mybir
from concourse.masks import make_identity

BF16, F32, U16 = mybir.dt.bfloat16, mybir.dt.float32, mybir.dt.uint16
SILU = mybir.ActivationFunctionType.Silu
MULT = mybir.AluOpType.mult

P = 128
TOKENS = 512
ENTRIES = 128
HIDDEN = 256
WARM_UPS = 3
BLOCKS = 2

FLOPS = 2 * 256 * HIDDEN * ENTRIES + 2 * HIDDEN * P * ENTRIES


def tile_rows_ffnback_silu_kernel(tc, base, x, w, b, w2, c, offs, out):
    nc = tc.nc
    with (
        tc.tile_pool(name="held", bufs=1) as held,
        tc.psum_pool(name="psum", bufs=1) as psum,
    ):
        w_tile = held.tile([P, BLOCKS, HIDDEN], BF16, name="w_tile")
        nc.sync.dma_start(w_tile[:], w.rearrange("e (p a) h -> p (e a) h", a=BLOCKS))
        x_tile = held.tile([P, BLOCKS, ENTRIES], BF16, name="x_tile")
        nc.sync.dma_start(x_tile[:], x.rearrange("(p a) n -> p a n", a=BLOCKS))
        b_row = held.tile([1, HIDDEN], F32, name="b_row")
        nc.scalar.dma_start(b_row[:], b.rearrange("h o -> o h"))
        c_row = held.tile([1, ENTRIES], F32, name="c_row")
        nc.scalar.dma_start(c_row[:], c)
        base_tile = held.tile([P, TOKENS], BF16, name="base_tile")
        nc.sync.dma_start(base_tile[:], base)
        w2_tile = held.tile([P, BLOCKS, P], BF16, name="w2_tile")
        nc.sync.dma_start(w2_tile[:], w2.rearrange("e (a p) m -> p (e a) m", p=P))
        offsets = held.tile([P, ENTRIES // 16], U16, name="offsets")
        nc.sync.dma_start(offsets[:], offs)

        identity = held.tile([P, P], BF16, name="identity")
        make_identity(nc, identity[:])

        ones = held.tile([1, P], F32, name="ones")
        nc.vector.memset(ones[:], 1.0)

        early = held.tile([1, P], F32, name="early")
        nc.scalar.activation(early[:], ones[:], SILU)

        b_columns = psum.tile([P, BLOCKS], F32, name="b_columns")
        for i in range(BLOCKS):
            nc.tensor.matmul(
                b_columns[:, i : i + 1], b_row[:, i * P : (i + 1) * P], ones[:, 0:1], start=True, stop=True
            )
        b_tile = held.tile([P, BLOCKS], F32, name="b_tile")
        nc.vector.tensor_copy(b_tile[:], b_columns[:])

        zeros = held.tile([P, TOKENS], BF16, name="zeros")
        nc.vector.memset(zeros[:], 0.0)
        warm = psum.tile([P, TOKENS], F32, name="warm")
        for step in range(WARM_UPS):
            nc.tensor.matmul(warm[:], zeros[:, 0:P], zeros[:], start=True, stop=True)

        c_all = psum.tile([P, ENTRIES], F32, name="c_all")
        nc.tensor.matmul(c_all[:], ones[:], c_row[:], start=True, stop=True)

        hidden = held.tile([P, BLOCKS, ENTRIES], BF16, name="hidden")
        for i in range(BLOCKS):
            pre = psum.tile([P, ENTRIES], F32, name=f"pre{i}")
            for k in range(BLOCKS):
                nc.tensor.matmul(
                    pre[:],
                    w_tile[:, k, i * P : (i + 1) * P],
                    x_tile[:, k, :],
                    start=(k == 0),
                    stop=(k == BLOCKS - 1),
                )
            act = held.tile([P, ENTRIES], F32, name=f"act{i}")
            nc.scalar.activation(act[:], pre[:], SILU, bias=b_tile[:, i : i + 1])
            nc.vector.tensor_tensor(hidden[:, i, :], act[:], c_all[:], MULT)

        window = psum.tile([P, TOKENS], F32, name="window")
        nc.tensor.matmul(window[:], identity[:], base_tile[:], start=True, stop=False)

        for i in range(BLOCKS):
            nc.tensor.matmul(
                window[:].indirect(offsets[:]),
                w2_tile[:, i, :],
                hidden[:, i, :],
                start=False,
                stop=(i == BLOCKS - 1),
            )

        z_tile = held.tile([P, TOKENS], F32, name="z_tile")
        nc.vector.tensor_copy(z_tile[:], window[:])
        nc.sync.dma_start(out, z_tile[:])
